import numpy as np, ml_dtypes
CORES = [15,47,79,175,207]
N = 5
import mx_ref
NC, K = 128, 3
CNT = [[0,8,40,48,32],[32,0,16,32,48],[80,0,0,40,8],[16,0,72,0,40],[0,120,0,8,0]]
OFF = [[sum(c[:e]) for e in range(N + 1)] for c in CNT]
BF = ml_dtypes.bfloat16
def setup_inputs(rng):
    def f(*shape):
        return mx_ref.flush((rng.standard_normal(shape, dtype=np.float32) * np.exp2(rng.integers(-2, 3, shape[:-1] + (1,)))).astype(BF))
    return {"x": f(N, 128, 4 * NC), "w": f(N, 128, 512)}
def setup_inputs_blocks(rng):
    d = setup_inputs(rng)
    for k in ("x", "w"): d[k] = mx_ref.spread(d[k], rng, 4)
    return d
def setup_inputs_wide(rng):
    d = setup_inputs(rng)
    for k in ("x", "w"): d[k] = mx_ref.flush((d[k].astype(np.float32) * np.exp2(rng.integers(-8, 9, (N, 1, 1))).astype(np.float32)).astype(BF))
    return d
def setup_inputs_zeros(rng):
    d = setup_inputs(rng); v = d["x"].reshape(N, 128, -1, 4).copy()
    v[np.broadcast_to((rng.random((N, 1, v.shape[2], 1)) < 0.33), v.shape)] = 0
    d["x"] = v.reshape(d["x"].shape)
    return d
def reference(x, w):
    y = np.zeros((N, 128, K * NC), np.float32)
    for e in range(N):
        t = np.concatenate([x[j][:, 4 * OFF[j][(e - k) % N]:4 * OFF[j][(e - k) % N + 1]] for k in range(K) for j in range(N)], axis=1)
        y[e] = mx_ref.matmul(mx_ref.quantize(w[e]), mx_ref.quantize(t))
    return {"y": y}

from concourse.mybir import dt, ActivationFunctionType

K = 3
NC = 128
COLS = 528
TILE = 176
MIN = 128

SCRATCH = {
    "xt": ("sbuf", [128, 4 * TILE], "bfloat16"),
    "wt": ("sbuf", [128, 512], "bfloat16"),
    "q": ("sbuf", [128, COLS], "float8_e4m3fn_x4"),
    "qs": ("sbuf", [128, COLS], "uint8"),
    "wq": ("sbuf", [128, 128], "float8_e4m3fn_x4"),
    "ws": ("sbuf", [128, 128], "uint8"),
    "yt": ("sbuf", [128, K * NC], "float32"),
    "ps": ("psum", [128, 512 * 4], "float32"),
}
SEMAPHORES = (["xload", "wload", "xq", "wq_done", "sent", "vcopy", "scopy", "stored"] + ["mm%d" % k for k in range(4)]
              + ["c%d" % s for s in range(5)] + ["p%d" % s for s in range(5)])

VIA = {(0, 4): 3, (1, 3): 4, (2, 3): 4, (4, 2): 1, (3, 1): 0}
TURN = {0: (1, 2, 3, 4, 1), 1: (2, 3, 4, 0, 2), 2: (3, 4, 0), 3: (4, 0, 2, 4), 4: (1, 3)}
ORDER = {0: (3, 2, 1), 1: (4, 0, 2), 2: (4, 0, 1), 3: (0, 2, 4), 4: (1, 0, 3)}
LAND = {0: ((3,), (4, 1, 2)), 1: ((4,), (2, 0)), 2: ((3, 0), (1,)), 3: ((0,), (4,)), 4: ((2, 1), (3,))}
AHEAD = {(3, 4), (4, 3)}

_plans = {}


def _window(cols, need):
    best = None
    have, a, left = {}, 0, len(need)
    for b, c in enumerate(cols):
        if c in need:
            have[c] = have.get(c, 0) + 1
            if have[c] == 1:
                left -= 1
        while left == 0:
            if best is None or b + 1 - a <= best[1] - best[0]:
                best = (a, b + 1)
            if cols[a] in need:
                have[cols[a]] -= 1
                if have[cols[a]] == 0:
                    left += 1
            a += 1
    return best


def _plan(T, topo):
    cnt, cores = T.tables["CNT"], T.cores
    n = len(cores)
    off = [[sum(r[:e]) for e in range(n + 1)] for r in cnt]

    def tokens(j, e):
        return [(j, t) for t in range(off[j][e], off[j][e + 1])]

    def wants(d, j):
        return {c for k in range(K) for c in tokens(j, (d - k) % n)}

    for (s, d), r in VIA.items():
        assert topo.host(cores[r]) == topo.host(cores[d]) != topo.host(cores[s])
    tile, base, cols = {}, {}, {}
    for j in range(n):
        tile[j] = [c for e in TURN[j] for c in tokens(j, e)]
        base[j] = -len(tile[j]) % 16
        cols[j] = [None] * base[j] + tile[j]
    end = {j: len(cols[j]) for j in range(n)}
    runs, place = {}, {}
    todo = [(s, d) for d in range(n) for g in LAND[d] for s in g]
    while todo:
        left = []
        for s, d in todo:
            own = set() if (s, d) in VIA else wants(d, s)
            for (q, d2), r in VIA.items():
                if (q, r) == (s, d):
                    own |= wants(d2, s)
            passed = {c for (q, d2), r in VIA.items() if (r, d2) == (s, d) for c in wants(d, q)}
            before = [(q, d) for g in LAND[d] for q in g]
            before = before[:before.index((s, d))]
            if any(p not in runs for p in before) or not (own | passed) <= set(cols[s]):
                left.append((s, d))
                continue
            runs[s, d] = _window(cols[s], own | passed)
            place[s, d] = len(cols[d])
            cols[d] += cols[s][runs[s, d][0]:runs[s, d][1]]
        assert len(left) < len(todo)
        todo = left
    for d in range(n):
        assert len(cols[d]) <= COLS and len(tile[d]) <= TILE
    goal = {e: [c for k in range(K) for j in range(n) for c in tokens(j, (e - k) % n)] for e in range(n)}
    return {"tile": tile, "base": base, "cols": cols, "end": end, "runs": runs, "place": place, "goal": goal}


def _groups(P, e):
    cols, pos = P["cols"][e], {}
    for i, c in enumerate(cols):
        pos.setdefault(c, i)
    pieces = []
    for i, c in enumerate(P["goal"][e]):
        p = pos[c]
        if pieces and pieces[-1][0] + pieces[-1][2] == p:
            pieces[-1][2] += 1
        else:
            pieces.append([p, i, 1])
    edges = [P["base"][e], P["end"][e]]
    for g in LAND[e]:
        edges.append(P["place"][g[-1], e] + P["runs"][g[-1], e][1] - P["runs"][g[-1], e][0])
    cut = []
    for p, i, w in pieces:
        for b in edges[1:]:
            if p < b < p + w:
                cut.append((p, i, b - p))
                p, i, w = b, i + b - p, p + w - b
        cut.append((p, i, w))
    return [[x for x in sorted(cut) if lo <= x[0] < hi] for lo, hi in zip(edges, edges[1:])]


def rank_program(g, core, T, topo):
    me = T.rank_of(core)
    if me is None:
        return
    if "p" not in _plans:
        _plans["p"] = _plan(T, topo)
    P = _plans["p"]
    sem, cores = T.sem, T.cores
    base, end, tile = P["base"][me], P["end"][me], P["tile"][me]
    relays = {s for (s, d), r in VIA.items() if r == me}

    def count(m):
        return bin(m).count("1")

    stretches = []
    for i, c in enumerate(tile):
        if stretches and stretches[-1][0] + stretches[-1][2] == c[1]:
            stretches[-1][2] += 1
        else:
            stretches.append([c[1], i, 1])
    stretches.sort(key=lambda s: -s[2])
    for k, (src, at, w) in enumerate(stretches):
        q = g.sync if k % 2 == 0 else g.scalar
        q.dma_start(T.xt[:, 4 * at:4 * (at + w)], T.x[:, 4 * src:4 * (src + w)]).then_inc(sem.xload, 16)
    g.scalar.dma_start(T.wt[:], T.w[:]).then_inc(sem.wload, 16)

    g.vector.wait_ge(sem.xload, 16 * len(stretches))
    g.vector.quantize_mx(T.q[:, base:end], T.qs[:, base:end], T.xt[:, :4 * (end - base)]).then_inc(sem.xq, 1)
    g.vector.wait_ge(sem.wload, 16)
    g.vector.quantize_mx(T.wq[:], T.ws[:], T.wt[:]).then_inc(sem.wq_done, 1)

    sent = [0]

    def send(dst, a, b, at, codes):
        rid, pid = topo.addr(cores[dst], core)
        assert topo.may_write(core, cores[dst]) and topo.same_plane(core, cores[dst])
        m = topo.mask(core, cores[dst])
        passes_on = any((s, r) == (me, dst) for (s, d), r in VIA.items())
        to = sem["c%d" % me] if codes or not passes_on else sem["p%d" % me]
        if codes:
            g.remote_dma(T.q[:, at:at + b - a].bitcast(dt.uint8), T.q[:, a:b].bitcast(dt.uint8), to, sem.sent, pid, rid, m)
        else:
            g.remote_dma(T.qs[:, at:at + b - a], T.qs[:, a:b], to, sem.sent, pid, rid, m)
        sent[0] += count(m)

    g.wait_ge(sem.xq, 1)
    for d in ORDER[me]:
        a, b = P["runs"][me, d]
        at = P["place"][me, d]
        if b <= end:
            send(d, a, b, at, True)
            send(d, a, b, at, False)
            continue
        sources = sorted(s for (s, x), r in VIA.items() if (x, r) == (d, me))
        lo = a
        if (me, d) in AHEAD:
            send(d, a, end, at, True)
            lo = end
        for s in sources:
            g.wait_ge(sem["c%d" % s], count(topo.mask(cores[s], core)))
        send(d, lo, b, at + lo - a, True)
        for s in sources:
            g.wait_ge(sem["p%d" % s], count(topo.mask(cores[s], core)))
        send(d, a, b, at, False)

    def cost(pieces):
        return sum(max(64, w) for _, _, w in pieces)

    first, early, last = _groups(P, me)
    half = min(range(len(last) + 1), key=lambda h: (abs(cost(last[:h]) - cost(last[h:])), h))
    banks = [(first, (), g.vector), (early, LAND[me][0], g.scalar), (last[:half], LAND[me][1], g.scalar), (last[half:], (), g.vector)]
    copies = {"v": 0, "s": 0}
    g.tensor.wait_ge(sem.xq, 1)
    g.tensor.wait_ge(sem.wq_done, 1)
    for k, (pieces, senders, queue) in enumerate(banks):
        for s in senders:
            ne = count(topo.mask(cores[s], core))
            if s in relays:
                g.tensor.wait_ge(sem["c%d" % s], ne)
                g.tensor.wait_ge(sem["p%d" % s], ne)
            else:
                g.tensor.wait_ge(sem["c%d" % s], ne * (3 if (s, me) in AHEAD else 2))
        if not pieces:
            continue
        if k == 0:
            lo, hi = base, end
        else:
            lo, hi = pieces[0][0], max(p + w for p, _, w in pieces)
            lo -= lo % 2
            hi += hi % 2
            lo = min(lo, hi - MIN)
        assert base <= lo and MIN <= hi - lo <= 512
        g.tensor.matmul_mx(T.ps[:, 512 * k:512 * k + hi - lo], T.wq[:], T.ws[:], T.q[:, lo:hi], T.qs[:, lo:hi],
                           True, True).then_inc(sem["mm%d" % k], 1)
        queue.wait_ge(sem["mm%d" % k], 1)
        for p, i, w in pieces:
            src = T.ps[:, 512 * k + p - lo:512 * k + p - lo + w]
            if queue is g.vector:
                g.vector.tensor_copy(T.yt[:, i:i + w], src).then_inc(sem.vcopy, 1)
                copies["v"] += 1
            else:
                g.scalar.activation(T.yt[:, i:i + w], src, ActivationFunctionType.Copy).then_inc(sem.scopy, 1)
                copies["s"] += 1

    if copies["v"]:
        g.sync.wait_ge(sem.vcopy, copies["v"])
    if copies["s"]:
        g.sync.wait_ge(sem.scopy, copies["s"])
    g.sync.dma_start(T.y[:], T.yt[:]).then_inc(sem.stored, 16)
    g.sync.wait_ge(sem.stored, 16)
    g.wait_ge(sem.sent, sent[0])
